import numpy as np
import ml_dtypes


def mxq(x, axis, fmt="e4m3"):
    dtype, down = {"e4m3": (ml_dtypes.float8_e4m3fn, 7), "e5m2": (ml_dtypes.float8_e5m2, 14)}[fmt]
    v = np.moveaxis(np.asarray(x, np.float32).astype(ml_dtypes.bfloat16).astype(np.float64), axis, -1)
    blocks = v.reshape(v.shape[:-1] + (-1, 32))
    amax = np.abs(blocks).max(-1, keepdims=True)
    byte = np.maximum(np.where(amax > 0, np.frexp(amax)[1] - 1 + 127, 0) - down, 1)
    scale = np.exp2(byte - 127.0)
    codes = (blocks / scale).astype(np.float32).astype(dtype).astype(np.float64)
    return np.moveaxis((codes * scale).reshape(v.shape), -1, axis)


WIDE = False


def mx_kscale(k):
    if not WIDE:
        return np.ones(k)
    levels = np.array([10, -10, 5, -5, 0])
    if k % 512:
        return np.exp2(np.random.permutation(np.resize(levels, k // 32))).repeat(32)
    a = np.empty((k // 512, 16))
    for p in range(k // 512):
        a[p, :8] = np.random.permutation(np.resize(levels, 8))
        for g in range(8):
            far = levels[np.abs(levels - a[p, g]) >= 10]
            a[p, g + 8] = far[np.random.randint(len(far))]
    return np.exp2(a.ravel()).repeat(32)


def f64(x):
    return np.asarray(x).astype(np.float64)


def striped(idx):
    return np.tile(np.asarray(idx).reshape(-1, 16).T, (8, 1)).astype(np.uint16)


def unstriped(offs):
    return offs[:16].T.reshape(-1).astype(np.int64)


E2M1 = np.array([0.0, 0.5, 1.0, 1.5, 2.0, 3.0, 4.0, 6.0, -0.0, -0.5, -1.0, -1.5, -2.0, -3.0, -4.0, -6.0])


def pack_weight(w, fmt):
    k, n = w.shape
    w = f64(np.asarray(w, np.float32).astype(ml_dtypes.bfloat16)).reshape(k // 32, 32, n)
    amax = np.abs(w).max(1)
    if fmt == "e4m3":
        byte = np.frexp(amax)[1] - 1 + 127 - 7
    else:
        mant, ex = np.frexp(amax / 6.0)
        byte = np.where(mant > 0.5, ex, ex - 1) + 127
    byte = np.clip(np.where(amax > 0, byte, 1), 1, 254)
    scaled = (w * np.exp2(127.0 - byte)[:, None, :]).reshape(k, n).astype(np.float32)
    by_word = np.ascontiguousarray(scaled.reshape(k // 512, 128, 4, n).transpose(0, 1, 3, 2))
    if fmt == "e4m3":
        words = by_word.astype(ml_dtypes.float8_e4m3fn).view(np.uint8)
    else:
        c = by_word.astype(ml_dtypes.float4_e2m1fn).view(np.uint8) & 0xF
        words = (c[..., 0::2] | (c[..., 1::2] << 4)).reshape(k // 512, 128, 2 * n)
    return np.ascontiguousarray(words), np.ascontiguousarray(byte.astype(np.uint8).reshape(k // 512, 16, n))


def unpack_weight(words, scales, fmt):
    g, _, n = scales.shape
    words = np.ascontiguousarray(words).reshape(g, 128, n, -1)
    if fmt == "e4m3":
        vals = words.view(ml_dtypes.float8_e4m3fn).astype(np.float64)
    else:
        nib = np.empty((g, 128, n, 4), np.uint8)
        nib[..., 0::2] = words & 0xF
        nib[..., 1::2] = words >> 4
        vals = E2M1[nib]
    vals = vals * np.repeat(np.exp2(scales.astype(np.float64) - 127.0), 8, axis=1)[..., None]
    return vals.transpose(0, 1, 3, 2).reshape(g * 512, n)


D, K, R, T, I, Q, G = 512, 512, 512, 2048, 512, 128, 64


def setup_inputs():
    n = np.random.standard_normal
    idx = np.random.permutation(T)[:I]
    fd = mx_kscale(D)
    fk = mx_kscale(K)
    fr = mx_kscale(R)
    keysp = pack_weight(n((D, T)) / fd[:, None], "e4m3")
    tabp = pack_weight(n((K, T)) / fk[:, None], "e4m3")
    return {
        "query": (n((D, Q)) * 0.6 / np.sqrt(D) * fd[:, None]).astype(np.float32),
        "keys_words": keysp[0],
        "keys_scales": keysp[1],
        "sharp": (np.random.uniform(1.0, 3.0, (Q, 1))).astype(np.float32),
        "tab_words": tabp[0],
        "tab_scales": tabp[1],
        "w1": (n((K, R)) * 1 / np.sqrt(K) * fk[:, None]).astype(np.float32),
        "temper": (np.random.uniform(0.4, 1.0, (R, 1))).astype(np.float32),
        "gout": (n((R, Q)) * 1 / np.sqrt(R) * fr[:, None]).astype(np.float32),
        "hsc": (np.random.uniform(0.7, 1.4, (R, 1)) / fr[:, None]).astype(np.float32),
        "old": (0.5 * n((Q, T))).astype(np.float32),
        "offs": striped(idx),
    }


def reference(query, keys_words, keys_scales, sharp, tab_words, tab_scales, w1, temper, gout, hsc, old, offs):
    idx = unstriped(offs)
    keysu = unpack_weight(keys_words, keys_scales, "e4m3")
    tabu = unpack_weight(tab_words, tab_scales, "e4m3")
    queryq = mxq(f64(query), 0, "e4m3")
    keysidxg = keysu[:, idx]
    a = queryq.T @ keysidxg
    p = np.exp(a)
    s = p.reshape(Q, G, I // G).sum(axis=2)
    ms = a.reshape(Q, G, I // G).mean(axis=2) * f64(sharp)
    pg = np.exp(ms - np.max(ms, axis=1, keepdims=True))
    z = np.sum(pg, axis=1, keepdims=True)
    sh = pg / z / s
    rr = np.repeat(sh, I // G, axis=1)
    w1q = mxq(f64(w1), 0, "e4m3")
    tabidxg = tabu[:, idx]
    zh = w1q.T @ tabidxg
    ht = np.exp(zh * f64(temper))
    mz = ht.reshape(R, G, I // G).sum(axis=2)
    mzr = np.repeat(mz, I // G, axis=1)
    hv = ht / mzr * 4.0
    hs1 = hv * f64(hsc)
    goutq = mxq(f64(gout), 0, "e4m3")
    hs1q = mxq(hs1, 0, "e4m3")
    c0 = goutq.T @ hs1q
    drr = c0 * p
    dsh = drr.reshape(Q, G, I // G).sum(axis=2)
    dz = np.sum(dsh / s * pg / np.square(z) * (-1.0), axis=1, keepdims=True)
    dpg = dsh / s / z + dz
    dms = dpg * pg
    e1 = dms * f64(sharp) / 8.0
    r1 = np.repeat(e1, I // G, axis=1)
    ds = dsh * pg / z / np.square(s) * (-1.0)
    r2 = np.repeat(ds, I // G, axis=1)
    dp = c0 * rr + r2
    da = r1 + dp * p
    gs = da * 512.0
    gf = np.zeros((Q, T))
    gf[:, idx] = gs
    y = f64(old) + gf
    return y

from contextlib import ExitStack

import concourse.mybir as mybir
from concourse.masks import make_identity

F32 = mybir.dt.float32
BF16 = mybir.dt.bfloat16
I32 = mybir.dt.int32
U32 = mybir.dt.uint32
U16 = mybir.dt.uint16
U8 = mybir.dt.uint8
FP8X4 = mybir.dt.float8_e4m3fn_x4
ALU = mybir.AluOpType
ACT = mybir.ActivationFunctionType
AXIS_X = mybir.AxisListType.X

P = 128
PACK = 4
D, R, T, I, Q, G = 512, 512, 2048, 512, 128, 64
J = I // G
HALVES = 2
IH = I // HALVES
GH = G // HALVES
OUT_CHUNK = 512

FLOPS = 2 * D * Q * I + 2 * D * R * I + 2 * R * Q * I


def tile_attend_blrshared_bygroup_kernel(
    tc, query, keys_words, keys_scales, sharp, tab_words, tab_scales, w1, temper, gout, hsc, old, offs, out
):
    nc = tc.nc
    with ExitStack() as ctx:
        lists = ctx.enter_context(tc.tile_pool(name="lists", bufs=1))
        sb = ctx.enter_context(tc.tile_pool(name="sb", bufs=1))
        ps = ctx.enter_context(tc.psum_pool(name="ps", bufs=1))

        def new(name, shape, dtype):
            return sb.tile(shape, dtype, name=name, align_bytes=64)

        offsets = lists.tile([P, I // 16], U16, name="offsets")
        tab_pool = new("tab_pool", [P, T], U32)
        key_pool = new("key_pool", [P, T], U32)
        tab_spool = new("tab_spool", [P, T], U8)
        key_spool = new("key_spool", [P, T], U8)
        w_raw = new("w_raw", [P, PACK, R], F32)
        q_raw = new("q_raw", [P, PACK, Q], F32)
        g_raw = new("g_raw", [P, PACK, Q], F32)
        old_sb = new("old_sb", [P, T], F32)
        sharp_sb = new("sharp_sb", [P, 1], F32)
        temper_sb = new("temper_sb", [P, PACK], F32)
        hsc_sb = new("hsc_sb", [P, PACK], F32)
        window = new("window", [P, T], F32)

        nc.gpsimd.memset(tab_spool[:].bitcast(I32), 0)
        nc.vector.memset(key_spool[:].bitcast(I32), 0)

        def load_words(dst, src):
            nc.sync.dma_start(dst[:].bitcast(I32), src[0].rearrange("p n t -> p (n t)").bitcast(I32))

        def load_scales(eng, dst, src):
            for quad in range(4):
                eng.dma_start(
                    dst[32 * quad : 32 * quad + 4, :].bitcast(I32), src[0, 4 * quad : 4 * quad + 4, :].bitcast(I32)
                )

        nc.sync.dma_start(w_raw[:], w1.rearrange("(p j) r -> p j r", j=PACK))
        load_scales(nc.sync, tab_spool, tab_scales)
        nc.sync.dma_start(offsets[:], offs)
        load_words(tab_pool, tab_words)
        nc.sync.dma_start(q_raw[:], query.rearrange("(p j) q -> p j q", j=PACK))
        load_scales(nc.sync, key_spool, keys_scales)
        load_words(key_pool, keys_words)
        nc.sync.dma_start(g_raw[:], gout.rearrange("(p j) q -> p j q", j=PACK))
        nc.sync.dma_start(old_sb[:], old)
        nc.gpsimd.dma_start(temper_sb[:], temper.rearrange("(p t) o -> p (t o)", t=PACK))
        nc.gpsimd.dma_start(hsc_sb[:], hsc.rearrange("(p t) o -> p (t o)", t=PACK))
        nc.gpsimd.dma_start(sharp_sb[:], sharp)

        ident = new("ident", [P, P], F32)
        make_identity(nc, ident[:])
        warm = new("warm", [P, 1], F32)
        warm_out = new("warm_out", [P, 1], F32)
        nc.vector.memset(warm[:], 0.0)
        nc.scalar.activation(warm_out[:], warm[:], ACT.Exp)
        nc.vector.memset(window[:], 0.0)

        tab_s = new("tab_s", [P, I], U8)
        nc.vector.tensor_copy(tab_s[:], tab_spool[:].indirect(offsets[:]))

        w_bf = new("w_bf", [P, PACK, P, PACK], BF16)
        M_VEC = 80
        w_dst = w_bf[:].rearrange("p t m j -> p m j t")
        w_src = w_raw[:].rearrange("p j (m t) -> p m j t", t=PACK)
        nc.vector.tensor_copy(w_dst[:, :M_VEC], w_src[:, :M_VEC])
        nc.scalar.copy(w_dst[:, M_VEC:], w_src[:, M_VEC:])
        w_codes = new("w_codes", [P, R], U32)
        w_scales = new("w_scales", [P, R], U8)
        nc.vector.quantize_mx(w_codes[:].bitcast(FP8X4), w_scales[:], w_bf[:].rearrange("p t m j -> p (t m j)"))

        tab_g = []
        for h in range(HALVES):
            g = new("tab_g%d" % h, [P, IH], U32)
            nc.vector.tensor_copy(g[:], tab_pool[:].indirect(offsets[:, h * IH // 16 : (h + 1) * IH // 16]))
            tab_g.append(g)

        def cast_rows(name, raw, on_scalar):
            bf = new(name, [P, Q, PACK], BF16)
            dst = bf[:].rearrange("p (c i) j -> p c j i", i=4)
            src = raw[:].rearrange("p j (c i) -> p c j i", i=4)
            if on_scalar:
                nc.scalar.copy(dst, src)
            else:
                nc.gpsimd.tensor_scalar(dst, src, 1.0, 0.0, ALU.mult, ALU.add)
            return bf

        def quantize(name, bf, width):
            codes = new(name + "_codes", [P, width], U32)
            scales = new(name + "_scales", [P, width], U8)
            nc.vector.quantize_mx(codes[:].bitcast(FP8X4), scales[:], bf[:].rearrange("p c j -> p (c j)"))
            return codes, scales

        hsc4 = new("hsc4", [P, PACK], F32)
        nc.gpsimd.tensor_scalar(hsc4[:], hsc_sb[:], 4.0, 0.0, ALU.mult, ALU.add)
        nsharp8 = new("nsharp8", [P, 1], F32)
        nc.gpsimd.tensor_scalar(nsharp8[:], sharp_sb[:], -1.0 / J, 0.0, ALU.mult, ALU.add)

        def feature(tile, t):
            return tile[:].rearrange("p j (c t g) -> p t j c g", t=PACK, g=4)[:, t]

        q_bf = cast_rows("q_bf", q_raw, True)
        ht = []
        for h in range(HALVES):
            e = new("ht%d" % h, [P, J, P], F32)
            for t in range(PACK):
                zh = ps.tile([P, IH], F32, name="zh", tag="product", bufs=3)
                nc.tensor.matmul_mx(
                    zh[:],
                    lhsT=w_codes[:, t * P : (t + 1) * P].bitcast(FP8X4),
                    lhsT_scale=w_scales[:, t * P : (t + 1) * P],
                    rhs=tab_g[h][:].bitcast(FP8X4),
                    rhs_scale=tab_s[:, h * IH : (h + 1) * IH],
                    start=True,
                    stop=True,
                )
                nc.scalar.activation(
                    feature(e, t),
                    zh[:].rearrange("p (c g j) -> p j c g", g=4, j=J),
                    ACT.Exp,
                    scale=temper_sb[:, t : t + 1],
                )
            ht.append(e)

        key_s = new("key_s", [P, I], U8)
        nc.vector.tensor_copy(key_s[:], key_spool[:].indirect(offsets[:]))
        q_codes, q_scales = quantize("q", q_bf, Q)
        key_g = new("key_g", [P, I], U32)
        nc.vector.tensor_copy(key_g[:], key_pool[:].indirect(offsets[:]))

        def group_sums(h):
            mz = ps.tile([P, P], F32, name="mz%d" % h)
            for j in range(J):
                nc.tensor.matmul(mz[:], ht[h][:, j, :], ident[:], start=j == 0, stop=j == J - 1, is_transpose=True)
            return mz

        def recips(h, mz):
            turned = new("turned%d" % h, [P, P], F32)
            nc.vector.reciprocal(turned[:], mz[:])
            rec = ps.tile([P, P], F32, name="rec%d" % h)
            nc.tensor.transpose(rec[:], turned[:], ident[:])
            return rec

        def scaled(h):
            hn = new("hn%d" % h, [P, J, P], F32)
            for t in range(PACK):
                nc.scalar.activation(feature(hn, t), feature(ht[h], t), ACT.Copy, scale=hsc4[:, t : t + 1])
            return hn

        def normalise(h, hn, rec):
            hs = new("hs%d" % h, [P, IH, PACK], BF16)
            nc.vector.tensor_tensor(
                hs[:].rearrange("p (j c g) t -> p j c t g", j=J, g=4),
                hn[:].rearrange("p j (c t g) -> p j c t g", t=PACK, g=4),
                rec[:].rearrange("p (c t g) -> p c t g", t=PACK, g=4).unsqueeze(1).to_broadcast([P, J, GH // 4, PACK, 4]),
                ALU.mult,
            )
            return hs

        def spread(ap, n):
            return ap.unsqueeze(2).to_broadcast([P, n, J])

        def grouped(ap):
            return ap.rearrange("p (g j) -> p g j", j=J)

        mz0 = group_sums(0)
        a = ps.tile([P, I], F32, name="a")
        nc.tensor.matmul_mx(
            a[:],
            lhsT=q_codes[:].bitcast(FP8X4),
            lhsT_scale=q_scales[:],
            rhs=key_g[:].bitcast(FP8X4),
            rhs_scale=key_s[:],
            start=True,
            stop=True,
        )
        mz1 = group_sums(1)
        p = new("p", [P, I], F32)
        nc.scalar.activation(p[:], a[:], ACT.Exp)
        hn0 = scaled(0)
        hn1 = scaled(1)

        rec0 = recips(0, mz0)
        asum = new("asum", [P, G], F32)
        nc.vector.tensor_reduce(asum[:], grouped(a[:]), AXIS_X, ALU.add)
        sz = new("sz", [P, G + 1], F32)
        nc.vector.tensor_reduce(sz[:, :G], grouped(p[:]), AXIS_X, ALU.add)
        nms = new("nms", [P, G], F32)
        nmax = new("nmax", [P, 1], F32)
        nc.vector.tensor_scalar(nms[:], asum[:], nsharp8[:], None, ALU.mult, ALU.min, accum_out=nmax[:])
        pg = new("pg", [P, G], F32)
        nc.scalar.activation(pg[:], nms[:], ACT.Exp, bias=nmax[:], scale=-1.0, accum_out=sz[:, G : G + 1])
        rec1 = recips(1, mz1)
        rsz = new("rsz", [P, G + 1], F32)
        nc.vector.reciprocal(rsz[:], sz[:])
        rz = rsz[:, G : G + 1]
        g_bf = cast_rows("g_bf", g_raw, True)
        share = new("share", [P, G], F32)
        nc.vector.scalar_tensor_tensor(share[:], pg[:], rz, rsz[:, :G], ALU.mult, ALU.mult)
        pi = new("pi", [P, G], F32)
        nc.scalar.activation(pi[:], pg[:], ACT.Copy, scale=rz)

        hs0 = normalise(0, hn0, rec0)
        wgt = new("wgt", [P, I], F32)
        nc.vector.tensor_tensor(grouped(wgt[:]), grouped(p[:]), spread(share[:], G), ALU.mult)
        g_codes, g_scales = quantize("g", g_bf, Q)
        h0_codes, h0_scales = quantize("h0", hs0, IH)
        hs1 = normalise(1, hn1, rec1)

        def second_product(h, codes, scales):
            c0 = ps.tile([P, IH], F32, name="c0", tag="product", bufs=3)
            nc.tensor.matmul_mx(
                c0[:],
                lhsT=g_codes[:].bitcast(FP8X4),
                lhsT_scale=g_scales[:],
                rhs=codes[:].bitcast(FP8X4),
                rhs_scale=scales[:],
                start=True,
                stop=True,
            )
            return c0

        t1 = new("t1", [P, I], F32)
        t2 = new("t2", [P, I], F32)
        t3 = new("t3", [P, I], F32)
        v = new("v", [P, G], F32)
        part = [new("part%d" % h, [P, 1], F32) for h in range(HALVES)]

        def weigh(h, c0):
            cols = slice(h * IH, (h + 1) * IH)
            nc.vector.scalar_tensor_tensor(
                grouped(t1[:, cols]),
                c0[:].rearrange("p (j g) -> p g j", j=J),
                512.0,
                grouped(wgt[:, cols]),
                ALU.mult,
                ALU.mult,
                accum_out=part[h][:],
            )

        def group_v(h):
            nc.vector.tensor_reduce(
                v[:, h * GH : (h + 1) * GH], grouped(t1[:, h * IH : (h + 1) * IH]), AXIS_X, ALU.add
            )

        nu = new("nu", [P, G], F32)

        def group_mean(h):
            gs = slice(h * GH, (h + 1) * GH)
            nc.vector.scalar_tensor_tensor(nu[:, gs], v[:, gs], -1.0, rsz[:, gs], ALU.mult, ALU.mult)

        def local_term(h):
            cols = slice(h * IH, (h + 1) * IH)
            nc.vector.tensor_tensor(
                grouped(t2[:, cols]), grouped(p[:, cols]), spread(nu[:, h * GH : (h + 1) * GH], GH), ALU.mult
            )

        c00 = second_product(0, h0_codes, h0_scales)
        weigh(0, c00)
        h1_codes, h1_scales = quantize("h1", hs1, IH)
        c01 = second_product(1, h1_codes, h1_scales)
        group_v(0)
        group_mean(0)
        weigh(1, c01)
        local_term(0)
        total = new("total", [P, 1], F32)
        group_v(1)
        nc.vector.tensor_tensor(total[:], part[0][:], part[1][:], ALU.add)
        group_mean(1)
        centred = new("centred", [P, G], F32)
        nc.vector.scalar_tensor_tensor(centred[:], pi[:], total[:], v[:], ALU.mult, ALU.subtract)
        local_term(1)
        nc.vector.scalar_tensor_tensor(
            grouped(t3[:]), spread(centred[:], G), nsharp8[:], grouped(t1[:]), ALU.mult, ALU.add
        )
        nc.vector.tensor_tensor(window[:].indirect(offsets[:]), t2[:], t3[:], ALU.add)

        for c in range(T // OUT_CHUNK):
            cols = slice(c * OUT_CHUNK, (c + 1) * OUT_CHUNK)
            res = new("res%d" % c, [P, OUT_CHUNK], F32)
            nc.vector.tensor_tensor(res[:], window[:, cols], old_sb[:, cols], ALU.add)
            nc.sync.dma_start(out[:, cols], res[:])
